import numpy as np
import ml_dtypes


def mxq(x, axis, fmt="e4m3"):
    dtype, down = {"e4m3": (ml_dtypes.float8_e4m3fn, 7), "e5m2": (ml_dtypes.float8_e5m2, 14)}[fmt]
    v = np.moveaxis(np.asarray(x, np.float32).astype(ml_dtypes.bfloat16).astype(np.float64), axis, -1)
    blocks = v.reshape(v.shape[:-1] + (-1, 32))
    amax = np.abs(blocks).max(-1, keepdims=True)
    byte = np.maximum(np.where(amax > 0, np.frexp(amax)[1] - 1 + 127, 0) - down, 1)
    scale = np.exp2(byte - 127.0)
    codes = (blocks / scale).astype(np.float32).astype(dtype).astype(np.float64)
    return np.moveaxis((codes * scale).reshape(v.shape), -1, axis)


WIDE = False


def mx_kscale(k):
    if not WIDE:
        return np.ones(k)
    levels = np.array([10, -10, 5, -5, 0])
    if k % 512:
        return np.exp2(np.random.permutation(np.resize(levels, k // 32))).repeat(32)
    a = np.empty((k // 512, 16))
    for p in range(k // 512):
        a[p, :8] = np.random.permutation(np.resize(levels, 8))
        for g in range(8):
            far = levels[np.abs(levels - a[p, g]) >= 10]
            a[p, g + 8] = far[np.random.randint(len(far))]
    return np.exp2(a.ravel()).repeat(32)


def f64(x):
    return np.asarray(x).astype(np.float64)


def striped8(idx):
    return np.asarray(idx).reshape(8, -1, 16).transpose(0, 2, 1).reshape(128, -1).astype(np.uint16)


def unstriped8(offs):
    return offs.reshape(8, 16, -1).transpose(0, 2, 1).reshape(8, -1).astype(np.int64)


def pick8(x, idx, run):
    r = np.arange(len(x))
    return x[r[:, None], idx[r % (8 * run) // run]]


E2M1 = np.array([0.0, 0.5, 1.0, 1.5, 2.0, 3.0, 4.0, 6.0, -0.0, -0.5, -1.0, -1.5, -2.0, -3.0, -4.0, -6.0])


def pack_weight(w, fmt):
    k, n = w.shape
    w = f64(np.asarray(w, np.float32).astype(ml_dtypes.bfloat16)).reshape(k // 32, 32, n)
    amax = np.abs(w).max(1)
    if fmt == "e4m3":
        byte = np.frexp(amax)[1] - 1 + 127 - 7
    else:
        mant, ex = np.frexp(amax / 6.0)
        byte = np.where(mant > 0.5, ex, ex - 1) + 127
    byte = np.clip(np.where(amax > 0, byte, 1), 1, 254)
    scaled = (w * np.exp2(127.0 - byte)[:, None, :]).reshape(k, n).astype(np.float32)
    by_word = np.ascontiguousarray(scaled.reshape(k // 512, 128, 4, n).transpose(0, 1, 3, 2))
    if fmt == "e4m3":
        words = by_word.astype(ml_dtypes.float8_e4m3fn).view(np.uint8)
    else:
        c = by_word.astype(ml_dtypes.float4_e2m1fn).view(np.uint8) & 0xF
        words = (c[..., 0::2] | (c[..., 1::2] << 4)).reshape(k // 512, 128, 2 * n)
    return np.ascontiguousarray(words), np.ascontiguousarray(byte.astype(np.uint8).reshape(k // 512, 16, n))


def unpack_weight(words, scales, fmt):
    g, _, n = scales.shape
    words = np.ascontiguousarray(words).reshape(g, 128, n, -1)
    if fmt == "e4m3":
        vals = words.view(ml_dtypes.float8_e4m3fn).astype(np.float64)
    else:
        nib = np.empty((g, 128, n, 4), np.uint8)
        nib[..., 0::2] = words & 0xF
        nib[..., 1::2] = words >> 4
        vals = E2M1[nib]
    vals = vals * np.repeat(np.exp2(scales.astype(np.float64) - 127.0), 8, axis=1)[..., None]
    return vals.transpose(0, 1, 3, 2).reshape(g * 512, n)


D, T, I, Q = 512, 1024, 512, 128


def setup_inputs():
    n = np.random.standard_normal
    idx = np.stack([np.random.permutation(T)[:I] for _ in range(8)])
    idx2 = np.stack([np.random.permutation(T)[:I] for _ in range(8)])
    fd = mx_kscale(D)
    keysp = pack_weight(n((D, T)) / fd[:, None], "e4m3")
    return {
        "query": (n((D, Q)) * 1.0 / np.sqrt(D) * fd[:, None]).astype(np.float32),
        "query2": (n((D, Q)) * 1.0 / np.sqrt(D) * fd[:, None]).astype(np.float32),
        "keys_words": keysp[0],
        "keys_scales": keysp[1],
        "lam": (np.random.uniform(1.0, 3.0, (Q, 1))).astype(np.float32),
        "smear": (np.random.uniform(0.3, 0.8, (Q, 1))).astype(np.float32),
        "old": (np.random.uniform(0.0, 2.0, (Q, T))).astype(np.float32),
        "fade": (np.random.uniform(0.3, 0.9, (Q, 1))).astype(np.float32),
        "offs": striped8(idx),
        "offs2": striped8(idx2),
    }


def reference(query, query2, keys_words, keys_scales, lam, smear, old, fade, offs, offs2):
    idx = unstriped8(offs)
    idx2 = unstriped8(offs2)
    keysu = unpack_weight(keys_words, keys_scales, "e4m3")
    queryq = mxq(f64(query), 0, "e4m3")
    a = queryq.T @ keysu
    query2q = mxq(f64(query2), 0, "e4m3")
    b = query2q.T @ keysu
    la = np.square(pick8(a, idx, 16)) + np.square(pick8(b, idx, 16))
    lb = np.square(pick8(a, idx2, 16)) + np.square(pick8(b, idx2, 16))
    s = (pick8(a, idx, 16) * pick8(a, idx2, 16) + pick8(b, idx, 16) * pick8(b, idx2, 16)) / np.sqrt(la * lb + 0.5) * f64(lam)
    p = np.exp(s - np.max(s, axis=1, keepdims=True))
    r = p / np.sum(p, axis=1, keepdims=True)
    r1 = np.pad(r, ((0, 0), (1, 0)))[:, :I]
    r2 = np.pad(r, ((0, 0), (2, 0)))[:, :I]
    w = r + r1 * f64(smear) + r2 * np.square(f64(smear))
    ws = w * 256.0
    wf = np.zeros((Q, T))
    wf[np.arange(Q)[:, None], idx[np.arange(Q) % 128 // 16]] = ws
    y = f64(old) * f64(fade) + wf
    return y

@@ -1,0 +1,182 @@
+from contextlib import ExitStack
+
+import concourse.mybir as mybir
+
+F32 = mybir.dt.float32
+BF16 = mybir.dt.bfloat16
+I32 = mybir.dt.int32
+U32 = mybir.dt.uint32
+U16 = mybir.dt.uint16
+U8 = mybir.dt.uint8
+FP8X4 = mybir.dt.float8_e4m3fn_x4
+ALU = mybir.AluOpType
+ACT = mybir.ActivationFunctionType
+AX = mybir.AxisListType
+
+P = 128
+D, T, SLOTS, Q = 512, 1024, 512, 128
+BANK = 512
+PAD = 8
+FLOPS = 2 * 2 * D * Q * T
+
+
+def tile_attend_planecos_smeared_counts_heads_kernel(
+    tc, query, query2, keys_words, keys_scales, lam, smear, old, fade, offs, offs2, out
+):
+    nc = tc.nc
+    with ExitStack() as ctx:
+        keep = ctx.enter_context(tc.tile_pool(name="keep", bufs=1))
+        psum = ctx.enter_context(tc.psum_pool(name="psum", bufs=1))
+
+        list1 = keep.tile([P, SLOTS // 16], U16, name="list1")
+        list2 = keep.tile([P, SLOTS // 16], U16, name="list2")
+
+        key_scales = keep.tile([P, T], U8, name="key_scales", align_bytes=64)
+        nc.gpsimd.memset(key_scales[:].bitcast(I32), 0)
+
+        raw = [keep.tile([P, 4, Q], F32, name="raw%d" % j, tag="raw%d" % j) for j in range(2)]
+        key_words = [keep.tile([P, BANK], U32, name="key_words%d" % h, align_bytes=64) for h in range(2)]
+        words_dram = keys_words[0].rearrange("p n t -> p (n t)")
+
+        def load_words(h):
+            nc.sync.dma_start(
+                out=key_words[h][:].bitcast(I32),
+                in_=words_dram[:, 4 * BANK * h : 4 * BANK * (h + 1)].bitcast(I32),
+            )
+
+        nc.sync.dma_start(out=raw[0][:], in_=query.rearrange("(p j) w -> p j w", j=4))
+        for quad in range(4):
+            nc.sync.dma_start(
+                out=key_scales[32 * quad : 32 * quad + 4, :].bitcast(I32),
+                in_=keys_scales[0, 4 * quad : 4 * quad + 4, :].bitcast(I32),
+            )
+        load_words(0)
+        nc.sync.dma_start(out=raw[1][:], in_=query2.rearrange("(p j) w -> p j w", j=4))
+        load_words(1)
+        nc.sync.dma_start(list1[:], offs)
+        nc.sync.dma_start(list2[:], offs2)
+        lam_sb = keep.tile([P, 1], F32, name="lam_sb")
+        smear_sb = keep.tile([P, 1], F32, name="smear_sb")
+        fade_sb = keep.tile([P, 1], F32, name="fade_sb")
+        nc.sync.dma_start(out=lam_sb[:], in_=lam)
+        nc.sync.dma_start(out=smear_sb[:], in_=smear)
+        nc.sync.dma_start(out=fade_sb[:], in_=fade)
+        old_sb = keep.tile([P, T], F32, name="old_sb")
+        nc.sync.dma_start(out=old_sb[:], in_=old)
+
+        placed = keep.tile([P, T], F32, name="placed")
+        nc.gpsimd.memset(placed[:], 0.0)
+        p_pad = keep.tile([P, PAD + SLOTS], F32, name="p_pad")
+        nc.gpsimd.memset(p_pad[:, 0:PAD], 0.0)
+
+        codes, scales = [], []
+        for j in range(2):
+            grouped = keep.tile([P, Q, 4], BF16, name="grouped%d" % j, align_bytes=64)
+            turned = raw[j][:].rearrange("p j w -> p w j")
+            nc.vector.tensor_copy(out=grouped[:, 0 : Q // 2, :], in_=turned[:, 0 : Q // 2, :])
+            nc.scalar.copy(out=grouped[:, Q // 2 : Q, :], in_=turned[:, Q // 2 : Q, :])
+            codes.append(keep.tile([P, Q], U32, name="codes%d" % j, align_bytes=64))
+            scales.append(keep.tile([P, Q], U8, name="scales%d" % j, align_bytes=64))
+            nc.vector.quantize_mx(
+                out=codes[j][:].bitcast(FP8X4), scales=scales[j][:], in_=grouped[:].rearrange("p w j -> p (w j)")
+            )
+
+        pieces = [(0, 512), (512, 768), (768, 1024)]
+        banks = {}
+        for j in range(2):
+            for lo, hi in pieces:
+                bank = psum.tile([P, hi - lo], F32, name="bank%d_%d" % (j, lo))
+                h = lo // BANK
+                nc.tensor.matmul_mx(
+                    out=bank[:],
+                    lhsT=codes[j][:].bitcast(FP8X4),
+                    lhsT_scale=scales[j][:],
+                    rhs=key_words[h][:, lo - BANK * h : hi - BANK * h].bitcast(FP8X4),
+                    rhs_scale=key_scales[:, lo:hi],
+                    start=True,
+                    stop=True,
+                )
+                banks[(j, lo)] = bank
+
+        def work(name):
+            return keep.tile([P, SLOTS], F32, name=name)
+
+        plane_a = keep.tile([P, T], F32, name="plane_a", tag="raw1")
+        plane_b = keep.tile([P, T], F32, name="plane_b")
+        nc.scalar.copy(out=plane_a[:, 0:512], in_=banks[(0, 0)][:])
+        nc.vector.tensor_copy(out=plane_a[:, 512:768], in_=banks[(0, 512)][:])
+        nc.scalar.copy(out=plane_a[:, 768:1024], in_=banks[(0, 768)][:])
+        for lo, hi in pieces:
+            nc.vector.tensor_copy(out=plane_b[:, lo:hi], in_=banks[(1, lo)][:])
+
+        a1, a2, b1, b2 = work("a1"), work("a2"), work("b1"), work("b2")
+        sa1, sa2, sb1, sb2 = work("sa1"), work("sa2"), work("sb1"), work("sb2")
+        halves = [slice(0, SLOTS // 2), slice(SLOTS // 2, SLOTS)]
+        nc.scalar.activation(a1[:], plane_a[:].indirect(list1[:]), ACT.Copy)
+        nc.scalar.activation(a2[:], plane_a[:].indirect(list2[:]), ACT.Copy)
+        nc.vector.tensor_copy(b1[:], plane_b[:].indirect(list1[:]))
+        nc.vector.tensor_copy(b2[:, halves[0]], plane_b[:].indirect(list2[:, 0:16]))
+        nc.scalar.activation(sa1[:], a1[:], ACT.Square)
+        nc.scalar.activation(b2[:, halves[1]], plane_b[:].indirect(list2[:, 16:32]), ACT.Copy)
+        nc.scalar.activation(sb1[:], b1[:], ACT.Square)
+        nc.scalar.activation(sa2[:], a2[:], ACT.Square)
+        for hs in halves:
+            nc.scalar.activation(sb2[:, hs], b2[:, hs], ACT.Square)
+        la, lb, den, rs = work("la"), work("lb"), work("den"), work("rs")
+        pb, s = work("pb"), work("s")
+        pa, dot = a1, la
+        nc.vector.tensor_tensor(pa[:], a1[:], a2[:], ALU.mult)
+        nc.vector.tensor_tensor(pb[:], b1[:], b2[:], ALU.mult)
+        nc.vector.tensor_tensor(la[:], sa1[:], sb1[:], ALU.add)
+        for hs in halves:
+            nc.vector.tensor_tensor(lb[:, hs], sa2[:, hs], sb2[:, hs], ALU.add)
+        for hs in halves:
+            nc.vector.tensor_tensor(den[:, hs], la[:, hs], lb[:, hs], ALU.mult)
+            nc.scalar.activation(rs[:, hs], den[:, hs], ACT.Abs_reciprocal_sqrt, bias=0.5)
+        for hs in halves:
+            nc.vector.tensor_tensor(dot[:, hs], pa[:, hs], pb[:, hs], ALU.add)
+        for hs in halves:
+            nc.vector.scalar_tensor_tensor(s[:, hs], dot[:, hs], lam_sb[:], rs[:, hs], ALU.mult, ALU.mult)
+        neg_max = keep.tile([P, 1], F32, name="neg_max")
+        nc.vector.tensor_reduce(neg_max[:], s[:], AX.X, ALU.max, negate=True)
+        total = keep.tile([P, 1], F32, name="total")
+        nc.scalar.activation(p_pad[:, PAD:], s[:], ACT.Exp, bias=neg_max[:], accum_out=total[:])
+
+        factors = keep.tile([P, 2], F32, name="factors")
+        nc.gpsimd.memset(factors[:, 0:1], 256.0)
+        nc.gpsimd.tensor_scalar(factors[:, 1:2], smear_sb[:], smear_sb[:], 256.0, ALU.mult, ALU.mult)
+        inv = keep.tile([P, 1], F32, name="inv")
+        normed = keep.tile([P, 2], F32, name="normed")
+        near = work("near")
+        half = SLOTS // 2
+
+        def make_near(c):
+            lo = PAD + half * c
+            nc.vector.scalar_tensor_tensor(
+                near[:, halves[c]], p_pad[:, lo - 1 : lo - 1 + half], smear_sb[:], p_pad[:, lo : lo + half],
+                ALU.mult, ALU.add,
+            )
+
+        nc.vector.reciprocal(inv[:], total[:])
+        make_near(0)
+        for c in range(2):
+            x = keep.tile([P, half], F32, name="x%d" % c)
+            y = keep.tile([P, half], F32, name="y%d" % c)
+            src_y = p_pad[:, PAD - 2 + half * c : PAD - 2 + half * (c + 1)]
+            if c == 0:
+                nc.vector.tensor_scalar(y[:], src_y, inv[:], factors[:, 1:2], ALU.mult, ALU.mult)
+                nc.vector.tensor_scalar(normed[:], factors[:], inv[:], None, ALU.mult)
+                nc.vector.tensor_scalar(x[:], near[:, halves[c]], inv[:], 256.0, ALU.mult, ALU.mult)
+                make_near(1)
+            else:
+                nc.scalar.activation(x[:], near[:, halves[c]], ACT.Copy, scale=normed[:, 0:1])
+                nc.scalar.activation(y[:], src_y, ACT.Copy, scale=normed[:, 1:2])
+            nc.vector.tensor_tensor(placed[:].indirect(list1[:, 16 * c : 16 * (c + 1)]), x[:], y[:], ALU.add)
+
+        width = T // 4
+        for c in range(4):
+            cols = slice(width * c, width * (c + 1))
+            result = keep.tile([P, width], F32, name="result%d" % c)
+            nc.vector.scalar_tensor_tensor(result[:], old_sb[:, cols], fade_sb[:], placed[:, cols], ALU.mult, ALU.add)
+            queue = nc.sync if c % 2 == 0 else nc.scalar
+            queue.dma_start(out=out[:, cols], in_=result[:])

@@ -32,7 +32,7 @@ def tile_attend_planecos_smeared_counts_heads_kernel(
         list2 = keep.tile([P, SLOTS // 16], U16, name="list2")
 
         key_scales = keep.tile([P, T], U8, name="key_scales", align_bytes=64)
-        nc.gpsimd.memset(key_scales[:].bitcast(I32), 0)
+        nc.vector.memset(key_scales[:].bitcast(I32), 0)
 
         raw = [keep.tile([P, 4, Q], F32, name="raw%d" % j, tag="raw%d" % j) for j in range(2)]
         key_words = [keep.tile([P, BANK], U32, name="key_words%d" % h, align_bytes=64) for h in range(2)]
@@ -45,12 +45,12 @@ def tile_attend_planecos_smeared_counts_heads_kernel(
             )
 
         nc.sync.dma_start(out=raw[0][:], in_=query.rearrange("(p j) w -> p j w", j=4))
+        load_words(0)
         for quad in range(4):
             nc.sync.dma_start(
                 out=key_scales[32 * quad : 32 * quad + 4, :].bitcast(I32),
                 in_=keys_scales[0, 4 * quad : 4 * quad + 4, :].bitcast(I32),
             )
-        load_words(0)
         nc.sync.dma_start(out=raw[1][:], in_=query2.rearrange("(p j) w -> p j w", j=4))
         load_words(1)
         nc.sync.dma_start(list1[:], offs)
@@ -65,9 +65,9 @@ def tile_attend_planecos_smeared_counts_heads_kernel(
         nc.sync.dma_start(out=old_sb[:], in_=old)
 
         placed = keep.tile([P, T], F32, name="placed")
-        nc.gpsimd.memset(placed[:], 0.0)
+        nc.vector.memset(placed[:], 0.0)
         p_pad = keep.tile([P, PAD + SLOTS], F32, name="p_pad")
-        nc.gpsimd.memset(p_pad[:, 0:PAD], 0.0)
+        nc.vector.memset(p_pad[:, 0:PAD], 0.0)
 
         codes, scales = [], []
         for j in range(2):

@@ -34,6 +34,11 @@ def tile_attend_planecos_smeared_counts_heads_kernel(
         key_scales = keep.tile([P, T], U8, name="key_scales", align_bytes=64)
         nc.vector.memset(key_scales[:].bitcast(I32), 0)
 
+        warm = keep.tile([P, 1], F32, name="warm")
+        warm_out = keep.tile([P, 1], F32, name="warm_out")
+        nc.gpsimd.memset(warm[:], 1.0)
+        nc.scalar.activation(warm_out[:], warm[:], ACT.Abs_reciprocal_sqrt)
+
         raw = [keep.tile([P, 4, Q], F32, name="raw%d" % j, tag="raw%d" % j) for j in range(2)]
         key_words = [keep.tile([P, BANK], U32, name="key_words%d" % h, align_bytes=64) for h in range(2)]
         words_dram = keys_words[0].rearrange("p n t -> p (n t)")

@@ -86,10 +86,10 @@ def tile_attend_planecos_smeared_counts_heads_kernel(
                 out=codes[j][:].bitcast(FP8X4), scales=scales[j][:], in_=grouped[:].rearrange("p w j -> p (w j)")
             )
 
-        pieces = [(0, 512), (512, 768), (768, 1024)]
+        pieces = [[(0, 512), (512, 768), (768, 1024)], [(0, 256), (256, 512), (512, 768), (768, 1024)]]
         banks = {}
         for j in range(2):
-            for lo, hi in pieces:
+            for lo, hi in pieces[j]:
                 bank = psum.tile([P, hi - lo], F32, name="bank%d_%d" % (j, lo))
                 h = lo // BANK
                 nc.tensor.matmul_mx(
@@ -111,7 +111,7 @@ def tile_attend_planecos_smeared_counts_heads_kernel(
         nc.scalar.copy(out=plane_a[:, 0:512], in_=banks[(0, 0)][:])
         nc.vector.tensor_copy(out=plane_a[:, 512:768], in_=banks[(0, 512)][:])
         nc.scalar.copy(out=plane_a[:, 768:1024], in_=banks[(0, 768)][:])
-        for lo, hi in pieces:
+        for lo, hi in pieces[1]:
             nc.vector.tensor_copy(out=plane_b[:, lo:hi], in_=banks[(1, lo)][:])
 
         a1, a2, b1, b2 = work("a1"), work("a2"), work("b1"), work("b2")
@@ -121,7 +121,7 @@ def tile_attend_planecos_smeared_counts_heads_kernel(
         nc.scalar.activation(a2[:], plane_a[:].indirect(list2[:]), ACT.Copy)
         nc.vector.tensor_copy(b1[:], plane_b[:].indirect(list1[:]))
         nc.vector.tensor_copy(b2[:, halves[0]], plane_b[:].indirect(list2[:, 0:16]))
-        nc.scalar.activation(sa1[:], a1[:], ACT.Square)
+        nc.gpsimd.tensor_tensor(sa1[:], a1[:], a1[:], ALU.mult)
         nc.scalar.activation(b2[:, halves[1]], plane_b[:].indirect(list2[:, 16:32]), ACT.Copy)
         nc.scalar.activation(sb1[:], b1[:], ACT.Square)
         nc.scalar.activation(sa2[:], a2[:], ACT.Square)

@@ -11,12 +11,22 @@ U8 = mybir.dt.uint8
 FP8X4 = mybir.dt.float8_e4m3fn_x4
 ALU = mybir.AluOpType
 ACT = mybir.ActivationFunctionType
-AX = mybir.AxisListType
+AXIS = mybir.AxisListType
 
 P = 128
 D, T, SLOTS, Q = 512, 1024, 512, 128
-BANK = 512
+PACK = 4
+PER_COLUMN = 16
+STRETCH = 256
+STRETCHES = T // STRETCH
+KEY_LOAD = T // 2
+HALF = SLOTS // 2
 PAD = 8
+SMEAR_REACH = 2
+WEIGHT_SCALE = 256.0
+ROOT_FLOOR = 0.5
+STORES = 4
+
 FLOPS = 2 * 2 * D * Q * T
 
 
@@ -28,35 +38,36 @@ def tile_attend_planecos_smeared_counts_heads_kernel(
         keep = ctx.enter_context(tc.tile_pool(name="keep", bufs=1))
         psum = ctx.enter_context(tc.psum_pool(name="psum", bufs=1))
 
-        list1 = keep.tile([P, SLOTS // 16], U16, name="list1")
-        list2 = keep.tile([P, SLOTS // 16], U16, name="list2")
+        list1 = keep.tile([P, SLOTS // PER_COLUMN], U16, name="list1")
+        list2 = keep.tile([P, SLOTS // PER_COLUMN], U16, name="list2")
 
-        key_scales = keep.tile([P, T], U8, name="key_scales", align_bytes=64)
+        key_scales = keep.tile([P, STRETCH], U8, name="key_scales", align_bytes=64)
         nc.vector.memset(key_scales[:].bitcast(I32), 0)
 
-        warm = keep.tile([P, 1], F32, name="warm")
+        warm_in = keep.tile([P, 1], F32, name="warm_in")
         warm_out = keep.tile([P, 1], F32, name="warm_out")
-        nc.gpsimd.memset(warm[:], 1.0)
-        nc.scalar.activation(warm_out[:], warm[:], ACT.Abs_reciprocal_sqrt)
+        nc.gpsimd.memset(warm_in[:], 1.0)
+        nc.scalar.activation(warm_out[:], warm_in[:], ACT.Abs_reciprocal_sqrt)
 
-        raw = [keep.tile([P, 4, Q], F32, name="raw%d" % j, tag="raw%d" % j) for j in range(2)]
-        key_words = [keep.tile([P, BANK], U32, name="key_words%d" % h, align_bytes=64) for h in range(2)]
+        raw = [keep.tile([P, PACK, Q], F32, name="raw%d" % m, tag="raw%d" % m) for m in range(2)]
+        key_words = [keep.tile([P, KEY_LOAD], U32, name="key_words%d" % h, align_bytes=64) for h in range(2)]
         words_dram = keys_words[0].rearrange("p n t -> p (n t)")
 
         def load_words(h):
             nc.sync.dma_start(
                 out=key_words[h][:].bitcast(I32),
-                in_=words_dram[:, 4 * BANK * h : 4 * BANK * (h + 1)].bitcast(I32),
+                in_=words_dram[:, PACK * KEY_LOAD * h : PACK * KEY_LOAD * (h + 1)].bitcast(I32),
             )
 
-        nc.sync.dma_start(out=raw[0][:], in_=query.rearrange("(p j) w -> p j w", j=4))
+        nc.sync.dma_start(out=raw[0][:], in_=query.rearrange("(p t) q -> p t q", t=PACK))
         load_words(0)
         for quad in range(4):
+            rows = keys_scales[0, 4 * quad : 4 * quad + 4, :].bitcast(I32)
             nc.sync.dma_start(
-                out=key_scales[32 * quad : 32 * quad + 4, :].bitcast(I32),
-                in_=keys_scales[0, 4 * quad : 4 * quad + 4, :].bitcast(I32),
+                out=key_scales[32 * quad : 32 * quad + 4 * STRETCHES, :].bitcast(I32),
+                in_=rows.rearrange("r (j c) -> j r c", j=STRETCHES),
             )
-        nc.sync.dma_start(out=raw[1][:], in_=query2.rearrange("(p j) w -> p j w", j=4))
+        nc.sync.dma_start(out=raw[1][:], in_=query2.rearrange("(p t) q -> p t q", t=PACK))
         load_words(1)
         nc.sync.dma_start(list1[:], offs)
         nc.sync.dma_start(list2[:], offs2)
@@ -72,116 +83,126 @@ def tile_attend_planecos_smeared_counts_heads_kernel(
         placed = keep.tile([P, T], F32, name="placed")
         nc.vector.memset(placed[:], 0.0)
         p_pad = keep.tile([P, PAD + SLOTS], F32, name="p_pad")
-        nc.vector.memset(p_pad[:, 0:PAD], 0.0)
+        nc.vector.memset(p_pad[:, PAD - SMEAR_REACH : PAD], 0.0)
 
         codes, scales = [], []
-        for j in range(2):
-            grouped = keep.tile([P, Q, 4], BF16, name="grouped%d" % j, align_bytes=64)
-            turned = raw[j][:].rearrange("p j w -> p w j")
+        for m in range(2):
+            grouped = keep.tile([P, Q, PACK], BF16, name="grouped%d" % m, align_bytes=64)
+            turned = raw[m][:].rearrange("p t q -> p q t")
             nc.vector.tensor_copy(out=grouped[:, 0 : Q // 2, :], in_=turned[:, 0 : Q // 2, :])
             nc.scalar.copy(out=grouped[:, Q // 2 : Q, :], in_=turned[:, Q // 2 : Q, :])
-            codes.append(keep.tile([P, Q], U32, name="codes%d" % j, align_bytes=64))
-            scales.append(keep.tile([P, Q], U8, name="scales%d" % j, align_bytes=64))
+            codes.append(keep.tile([P, Q], U32, name="codes%d" % m, align_bytes=64))
+            scales.append(keep.tile([P, Q], U8, name="scales%d" % m, align_bytes=64))
             nc.vector.quantize_mx(
-                out=codes[j][:].bitcast(FP8X4), scales=scales[j][:], in_=grouped[:].rearrange("p w j -> p (w j)")
+                out=codes[m][:].bitcast(FP8X4), scales=scales[m][:], in_=grouped[:].rearrange("p q t -> p (q t)")
             )
 
-        pieces = [[(0, 512), (512, 768), (768, 1024)], [(0, 256), (256, 512), (512, 768), (768, 1024)]]
-        banks = {}
-        for j in range(2):
-            for lo, hi in pieces[j]:
-                bank = psum.tile([P, hi - lo], F32, name="bank%d_%d" % (j, lo))
-                h = lo // BANK
+        banks = [[], []]
+        for m in range(2):
+            for j in range(STRETCHES):
+                bank = psum.tile([P, STRETCH], F32, name="bank%d_%d" % (m, j))
+                h, start = divmod(STRETCH * j, KEY_LOAD)
                 nc.tensor.matmul_mx(
                     out=bank[:],
-                    lhsT=codes[j][:].bitcast(FP8X4),
-                    lhsT_scale=scales[j][:],
-                    rhs=key_words[h][:, lo - BANK * h : hi - BANK * h].bitcast(FP8X4),
-                    rhs_scale=key_scales[:, lo:hi],
+                    lhsT=codes[m][:].bitcast(FP8X4),
+                    lhsT_scale=scales[m][:],
+                    rhs=key_words[h][:, start : start + STRETCH].bitcast(FP8X4),
+                    rhs_scale=key_scales[4 * j : P, :],
                     start=True,
                     stop=True,
                 )
-                banks[(j, lo)] = bank
+                banks[m].append(bank)
 
-        def work(name):
+        a_sb = keep.tile([P, T], F32, name="a_sb", tag="raw1")
+        b_sb = keep.tile([P, T], F32, name="b_sb")
+        for j in range(STRETCHES):
+            columns = slice(STRETCH * j, STRETCH * (j + 1))
+            if j == STRETCHES - 2:
+                nc.vector.tensor_copy(out=a_sb[:, columns], in_=banks[0][j][:])
+            else:
+                nc.scalar.copy(out=a_sb[:, columns], in_=banks[0][j][:])
+        for j in range(STRETCHES):
+            nc.vector.tensor_copy(out=b_sb[:, STRETCH * j : STRETCH * (j + 1)], in_=banks[1][j][:])
+
+        def slots_tile(name):
             return keep.tile([P, SLOTS], F32, name=name)
 
-        plane_a = keep.tile([P, T], F32, name="plane_a", tag="raw1")
-        plane_b = keep.tile([P, T], F32, name="plane_b")
-        nc.scalar.copy(out=plane_a[:, 0:512], in_=banks[(0, 0)][:])
-        nc.vector.tensor_copy(out=plane_a[:, 512:768], in_=banks[(0, 512)][:])
-        nc.scalar.copy(out=plane_a[:, 768:1024], in_=banks[(0, 768)][:])
-        for lo, hi in pieces[1]:
-            nc.vector.tensor_copy(out=plane_b[:, lo:hi], in_=banks[(1, lo)][:])
+        halves = [slice(0, HALF), slice(HALF, SLOTS)]
+        list_halves = [slice(0, HALF // PER_COLUMN), slice(HALF // PER_COLUMN, SLOTS // PER_COLUMN)]
 
-        a1, a2, b1, b2 = work("a1"), work("a2"), work("b1"), work("b2")
-        sa1, sa2, sb1, sb2 = work("sa1"), work("sa2"), work("sb1"), work("sb2")
-        halves = [slice(0, SLOTS // 2), slice(SLOTS // 2, SLOTS)]
-        nc.scalar.activation(a1[:], plane_a[:].indirect(list1[:]), ACT.Copy)
-        nc.scalar.activation(a2[:], plane_a[:].indirect(list2[:]), ACT.Copy)
-        nc.vector.tensor_copy(b1[:], plane_b[:].indirect(list1[:]))
-        nc.vector.tensor_copy(b2[:, halves[0]], plane_b[:].indirect(list2[:, 0:16]))
-        nc.gpsimd.tensor_tensor(sa1[:], a1[:], a1[:], ALU.mult)
-        nc.scalar.activation(b2[:, halves[1]], plane_b[:].indirect(list2[:, 16:32]), ACT.Copy)
-        nc.scalar.activation(sb1[:], b1[:], ACT.Square)
-        nc.scalar.activation(sa2[:], a2[:], ACT.Square)
-        for hs in halves:
-            nc.scalar.activation(sb2[:, hs], b2[:, hs], ACT.Square)
-        la, lb, den, rs = work("la"), work("lb"), work("den"), work("rs")
-        pb, s = work("pb"), work("s")
-        pa, dot = a1, la
-        nc.vector.tensor_tensor(pa[:], a1[:], a2[:], ALU.mult)
-        nc.vector.tensor_tensor(pb[:], b1[:], b2[:], ALU.mult)
-        nc.vector.tensor_tensor(la[:], sa1[:], sb1[:], ALU.add)
-        for hs in halves:
-            nc.vector.tensor_tensor(lb[:, hs], sa2[:, hs], sb2[:, hs], ALU.add)
-        for hs in halves:
-            nc.vector.tensor_tensor(den[:, hs], la[:, hs], lb[:, hs], ALU.mult)
-            nc.scalar.activation(rs[:, hs], den[:, hs], ACT.Abs_reciprocal_sqrt, bias=0.5)
-        for hs in halves:
-            nc.vector.tensor_tensor(dot[:, hs], pa[:, hs], pb[:, hs], ALU.add)
-        for hs in halves:
-            nc.vector.scalar_tensor_tensor(s[:, hs], dot[:, hs], lam_sb[:], rs[:, hs], ALU.mult, ALU.mult)
-        neg_max = keep.tile([P, 1], F32, name="neg_max")
-        nc.vector.tensor_reduce(neg_max[:], s[:], AX.X, ALU.max, negate=True)
-        total = keep.tile([P, 1], F32, name="total")
-        nc.scalar.activation(p_pad[:, PAD:], s[:], ACT.Exp, bias=neg_max[:], accum_out=total[:])
+        a1, a2, b1, b2 = slots_tile("a1"), slots_tile("a2"), slots_tile("b1"), slots_tile("b2")
+        a1_sq, a2_sq, b1_sq, b2_sq = slots_tile("a1_sq"), slots_tile("a2_sq"), slots_tile("b1_sq"), slots_tile("b2_sq")
+        nc.scalar.activation(a1[:], a_sb[:].indirect(list1[:]), ACT.Copy)
+        nc.scalar.activation(a2[:], a_sb[:].indirect(list2[:]), ACT.Copy)
+        nc.vector.tensor_copy(b1[:], b_sb[:].indirect(list1[:]))
+        nc.vector.tensor_copy(b2[:, halves[0]], b_sb[:].indirect(list2[:, list_halves[0]]))
+        nc.gpsimd.tensor_tensor(a1_sq[:], a1[:], a1[:], ALU.mult)
+        nc.scalar.activation(b2[:, halves[1]], b_sb[:].indirect(list2[:, list_halves[1]]), ACT.Copy)
+        nc.scalar.activation(b1_sq[:], b1[:], ACT.Square)
+        nc.scalar.activation(a2_sq[:], a2[:], ACT.Square)
+        for half in halves:
+            nc.scalar.activation(b2_sq[:, half], b2[:, half], ACT.Square)
 
-        factors = keep.tile([P, 2], F32, name="factors")
-        nc.gpsimd.memset(factors[:, 0:1], 256.0)
-        nc.gpsimd.tensor_scalar(factors[:, 1:2], smear_sb[:], smear_sb[:], 256.0, ALU.mult, ALU.mult)
-        inv = keep.tile([P, 1], F32, name="inv")
-        normed = keep.tile([P, 2], F32, name="normed")
-        near = work("near")
-        half = SLOTS // 2
-
-        def make_near(c):
-            lo = PAD + half * c
+        la, lb, lengths, inv_root = slots_tile("la"), slots_tile("lb"), slots_tile("lengths"), slots_tile("inv_root")
+        b_product, score = slots_tile("b_product"), slots_tile("score")
+        a_product, dot = a1, la
+        nc.vector.tensor_tensor(a_product[:], a1[:], a2[:], ALU.mult)
+        nc.vector.tensor_tensor(b_product[:], b1[:], b2[:], ALU.mult)
+        nc.vector.tensor_tensor(la[:], a1_sq[:], b1_sq[:], ALU.add)
+        for half in halves:
+            nc.vector.tensor_tensor(lb[:, half], a2_sq[:, half], b2_sq[:, half], ALU.add)
+        for half in halves:
+            nc.vector.tensor_tensor(lengths[:, half], la[:, half], lb[:, half], ALU.mult)
+            nc.scalar.activation(inv_root[:, half], lengths[:, half], ACT.Abs_reciprocal_sqrt, bias=ROOT_FLOOR)
+        for half in halves:
+            nc.vector.tensor_tensor(dot[:, half], a_product[:, half], b_product[:, half], ALU.add)
+        for half in halves:
             nc.vector.scalar_tensor_tensor(
-                near[:, halves[c]], p_pad[:, lo - 1 : lo - 1 + half], smear_sb[:], p_pad[:, lo : lo + half],
-                ALU.mult, ALU.add,
+                score[:, half], dot[:, half], lam_sb[:], inv_root[:, half], ALU.mult, ALU.mult
             )
 
-        nc.vector.reciprocal(inv[:], total[:])
-        make_near(0)
-        for c in range(2):
-            x = keep.tile([P, half], F32, name="x%d" % c)
-            y = keep.tile([P, half], F32, name="y%d" % c)
-            src_y = p_pad[:, PAD - 2 + half * c : PAD - 2 + half * (c + 1)]
-            if c == 0:
-                nc.vector.tensor_scalar(y[:], src_y, inv[:], factors[:, 1:2], ALU.mult, ALU.mult)
-                nc.vector.tensor_scalar(normed[:], factors[:], inv[:], None, ALU.mult)
-                nc.vector.tensor_scalar(x[:], near[:, halves[c]], inv[:], 256.0, ALU.mult, ALU.mult)
-                make_near(1)
-            else:
-                nc.scalar.activation(x[:], near[:, halves[c]], ACT.Copy, scale=normed[:, 0:1])
-                nc.scalar.activation(y[:], src_y, ACT.Copy, scale=normed[:, 1:2])
-            nc.vector.tensor_tensor(placed[:].indirect(list1[:, 16 * c : 16 * (c + 1)]), x[:], y[:], ALU.add)
+        neg_max = keep.tile([P, 1], F32, name="neg_max")
+        nc.vector.tensor_reduce(neg_max[:], score[:], AXIS.X, ALU.max, negate=True)
+        total = keep.tile([P, 1], F32, name="total")
+        nc.scalar.activation(p_pad[:, PAD:], score[:], ACT.Exp, bias=neg_max[:], accum_out=total[:])
 
-        width = T // 4
-        for c in range(4):
-            cols = slice(width * c, width * (c + 1))
+        factors = keep.tile([P, 2], F32, name="factors")
+        nc.gpsimd.memset(factors[:, 0:1], WEIGHT_SCALE)
+        nc.gpsimd.tensor_scalar(factors[:, 1:2], smear_sb[:], smear_sb[:], WEIGHT_SCALE, ALU.mult, ALU.mult)
+        inv_total = keep.tile([P, 1], F32, name="inv_total")
+        normed = keep.tile([P, 2], F32, name="normed")
+        near = slots_tile("near")
+        near_part = [keep.tile([P, HALF], F32, name="near_part%d" % c) for c in range(2)]
+        far_part = [keep.tile([P, HALF], F32, name="far_part%d" % c) for c in range(2)]
+
+        def p_back(c, steps):
+            return p_pad[:, PAD - steps + HALF * c : PAD - steps + HALF * (c + 1)]
+
+        def make_near(c):
+            nc.vector.scalar_tensor_tensor(near[:, halves[c]], p_back(c, 1), smear_sb[:], p_back(c, 0), ALU.mult, ALU.add)
+
+        def scatter(c):
+            nc.vector.tensor_tensor(
+                placed[:].indirect(list1[:, list_halves[c]]), near_part[c][:], far_part[c][:], ALU.add
+            )
+
+        nc.vector.reciprocal(inv_total[:], total[:])
+        make_near(0)
+        nc.vector.tensor_scalar(far_part[0][:], p_back(0, SMEAR_REACH), inv_total[:], factors[:, 1:2], ALU.mult, ALU.mult)
+        nc.vector.tensor_scalar(normed[:], factors[:], inv_total[:], None, ALU.mult)
+        nc.vector.tensor_scalar(near_part[0][:], near[:, halves[0]], inv_total[:], WEIGHT_SCALE, ALU.mult, ALU.mult)
+        make_near(1)
+        scatter(0)
+        nc.scalar.activation(near_part[1][:], near[:, halves[1]], ACT.Copy, scale=normed[:, 0:1])
+        nc.scalar.activation(far_part[1][:], p_back(1, SMEAR_REACH), ACT.Copy, scale=normed[:, 1:2])
+        scatter(1)
+
+        width = T // STORES
+        for c in range(STORES):
+            columns = slice(width * c, width * (c + 1))
             result = keep.tile([P, width], F32, name="result%d" % c)
-            nc.vector.scalar_tensor_tensor(result[:], old_sb[:, cols], fade_sb[:], placed[:, cols], ALU.mult, ALU.add)
+            nc.vector.scalar_tensor_tensor(
+                result[:], old_sb[:, columns], fade_sb[:], placed[:, columns], ALU.mult, ALU.add
+            )
             queue = nc.sync if c % 2 == 0 else nc.scalar
-            queue.dma_start(out=out[:, cols], in_=result[:])
+            queue.dma_start(out=out[:, columns], in_=result[:])

from contextlib import ExitStack

import concourse.mybir as mybir

F32 = mybir.dt.float32
BF16 = mybir.dt.bfloat16
I32 = mybir.dt.int32
U32 = mybir.dt.uint32
U16 = mybir.dt.uint16
U8 = mybir.dt.uint8
FP8X4 = mybir.dt.float8_e4m3fn_x4
ALU = mybir.AluOpType
ACT = mybir.ActivationFunctionType
AXIS = mybir.AxisListType

P = 128
D, T, SLOTS, Q = 512, 1024, 512, 128
PACK = 4
PER_COLUMN = 16
STRETCH = 256
STRETCHES = T // STRETCH
KEY_LOAD = T // 2
HALF = SLOTS // 2
PAD = 8
SMEAR_REACH = 2
WEIGHT_SCALE = 256.0
ROOT_FLOOR = 0.5
STORES = 4

FLOPS = 2 * 2 * D * Q * T


def tile_attend_planecos_smeared_counts_heads_kernel(
    tc, query, query2, keys_words, keys_scales, lam, smear, old, fade, offs, offs2, out
):
    nc = tc.nc
    with ExitStack() as ctx:
        keep = ctx.enter_context(tc.tile_pool(name="keep", bufs=1))
        psum = ctx.enter_context(tc.psum_pool(name="psum", bufs=1))

        list1 = keep.tile([P, SLOTS // PER_COLUMN], U16, name="list1")
        list2 = keep.tile([P, SLOTS // PER_COLUMN], U16, name="list2")

        key_scales = keep.tile([P, STRETCH], U8, name="key_scales", align_bytes=64)
        nc.vector.memset(key_scales[:].bitcast(I32), 0)

        warm_in = keep.tile([P, 1], F32, name="warm_in")
        warm_out = keep.tile([P, 1], F32, name="warm_out")
        nc.gpsimd.memset(warm_in[:], 1.0)
        nc.scalar.activation(warm_out[:], warm_in[:], ACT.Abs_reciprocal_sqrt)

        raw = [keep.tile([P, PACK, Q], F32, name="raw%d" % m, tag="raw%d" % m) for m in range(2)]
        key_words = [keep.tile([P, KEY_LOAD], U32, name="key_words%d" % h, align_bytes=64) for h in range(2)]
        words_dram = keys_words[0].rearrange("p n t -> p (n t)")

        def load_words(h):
            nc.sync.dma_start(
                out=key_words[h][:].bitcast(I32),
                in_=words_dram[:, PACK * KEY_LOAD * h : PACK * KEY_LOAD * (h + 1)].bitcast(I32),
            )

        nc.sync.dma_start(out=raw[0][:], in_=query.rearrange("(p t) q -> p t q", t=PACK))
        load_words(0)
        for quad in range(4):
            rows = keys_scales[0, 4 * quad : 4 * quad + 4, :].bitcast(I32)
            nc.sync.dma_start(
                out=key_scales[32 * quad : 32 * quad + 4 * STRETCHES, :].bitcast(I32),
                in_=rows.rearrange("r (j c) -> j r c", j=STRETCHES),
            )
        nc.sync.dma_start(out=raw[1][:], in_=query2.rearrange("(p t) q -> p t q", t=PACK))
        load_words(1)
        nc.sync.dma_start(list1[:], offs)
        nc.sync.dma_start(list2[:], offs2)
        lam_sb = keep.tile([P, 1], F32, name="lam_sb")
        smear_sb = keep.tile([P, 1], F32, name="smear_sb")
        fade_sb = keep.tile([P, 1], F32, name="fade_sb")
        nc.sync.dma_start(out=lam_sb[:], in_=lam)
        nc.sync.dma_start(out=smear_sb[:], in_=smear)
        nc.sync.dma_start(out=fade_sb[:], in_=fade)
        old_sb = keep.tile([P, T], F32, name="old_sb")
        nc.sync.dma_start(out=old_sb[:], in_=old)

        placed = keep.tile([P, T], F32, name="placed")
        nc.vector.memset(placed[:], 0.0)
        p_pad = keep.tile([P, PAD + SLOTS], F32, name="p_pad")
        nc.vector.memset(p_pad[:, PAD - SMEAR_REACH : PAD], 0.0)

        codes, scales = [], []
        for m in range(2):
            grouped = keep.tile([P, Q, PACK], BF16, name="grouped%d" % m, align_bytes=64)
            turned = raw[m][:].rearrange("p t q -> p q t")
            nc.vector.tensor_copy(out=grouped[:, 0 : Q // 2, :], in_=turned[:, 0 : Q // 2, :])
            nc.scalar.copy(out=grouped[:, Q // 2 : Q, :], in_=turned[:, Q // 2 : Q, :])
            codes.append(keep.tile([P, Q], U32, name="codes%d" % m, align_bytes=64))
            scales.append(keep.tile([P, Q], U8, name="scales%d" % m, align_bytes=64))
            nc.vector.quantize_mx(
                out=codes[m][:].bitcast(FP8X4), scales=scales[m][:], in_=grouped[:].rearrange("p q t -> p (q t)")
            )

        banks = [[], []]
        for m in range(2):
            for j in range(STRETCHES):
                bank = psum.tile([P, STRETCH], F32, name="bank%d_%d" % (m, j))
                h, start = divmod(STRETCH * j, KEY_LOAD)
                nc.tensor.matmul_mx(
                    out=bank[:],
                    lhsT=codes[m][:].bitcast(FP8X4),
                    lhsT_scale=scales[m][:],
                    rhs=key_words[h][:, start : start + STRETCH].bitcast(FP8X4),
                    rhs_scale=key_scales[4 * j : P, :],
                    start=True,
                    stop=True,
                )
                banks[m].append(bank)

        a_sb = keep.tile([P, T], F32, name="a_sb", tag="raw1")
        b_sb = keep.tile([P, T], F32, name="b_sb")
        for j in range(STRETCHES):
            columns = slice(STRETCH * j, STRETCH * (j + 1))
            if j == STRETCHES - 2:
                nc.vector.tensor_copy(out=a_sb[:, columns], in_=banks[0][j][:])
            else:
                nc.scalar.copy(out=a_sb[:, columns], in_=banks[0][j][:])
        for j in range(STRETCHES):
            nc.vector.tensor_copy(out=b_sb[:, STRETCH * j : STRETCH * (j + 1)], in_=banks[1][j][:])

        def slots_tile(name):
            return keep.tile([P, SLOTS], F32, name=name)

        halves = [slice(0, HALF), slice(HALF, SLOTS)]
        list_halves = [slice(0, HALF // PER_COLUMN), slice(HALF // PER_COLUMN, SLOTS // PER_COLUMN)]

        a1, a2, b1, b2 = slots_tile("a1"), slots_tile("a2"), slots_tile("b1"), slots_tile("b2")
        a1_sq, a2_sq, b1_sq, b2_sq = slots_tile("a1_sq"), slots_tile("a2_sq"), slots_tile("b1_sq"), slots_tile("b2_sq")
        nc.scalar.activation(a1[:], a_sb[:].indirect(list1[:]), ACT.Copy)
        nc.scalar.activation(a2[:], a_sb[:].indirect(list2[:]), ACT.Copy)
        nc.vector.tensor_copy(b1[:], b_sb[:].indirect(list1[:]))
        nc.vector.tensor_copy(b2[:, halves[0]], b_sb[:].indirect(list2[:, list_halves[0]]))
        nc.gpsimd.tensor_tensor(a1_sq[:], a1[:], a1[:], ALU.mult)
        nc.scalar.activation(b2[:, halves[1]], b_sb[:].indirect(list2[:, list_halves[1]]), ACT.Copy)
        nc.scalar.activation(b1_sq[:], b1[:], ACT.Square)
        nc.scalar.activation(a2_sq[:], a2[:], ACT.Square)
        for half in halves:
            nc.scalar.activation(b2_sq[:, half], b2[:, half], ACT.Square)

        la, lb, lengths, inv_root = slots_tile("la"), slots_tile("lb"), slots_tile("lengths"), slots_tile("inv_root")
        b_product, score = slots_tile("b_product"), slots_tile("score")
        a_product, dot = a1, la
        nc.vector.tensor_tensor(a_product[:], a1[:], a2[:], ALU.mult)
        nc.vector.tensor_tensor(b_product[:], b1[:], b2[:], ALU.mult)
        nc.vector.tensor_tensor(la[:], a1_sq[:], b1_sq[:], ALU.add)
        for half in halves:
            nc.vector.tensor_tensor(lb[:, half], a2_sq[:, half], b2_sq[:, half], ALU.add)
        for half in halves:
            nc.vector.tensor_tensor(lengths[:, half], la[:, half], lb[:, half], ALU.mult)
            nc.scalar.activation(inv_root[:, half], lengths[:, half], ACT.Abs_reciprocal_sqrt, bias=ROOT_FLOOR)
        for half in halves:
            nc.vector.tensor_tensor(dot[:, half], a_product[:, half], b_product[:, half], ALU.add)
        for half in halves:
            nc.vector.scalar_tensor_tensor(
                score[:, half], dot[:, half], lam_sb[:], inv_root[:, half], ALU.mult, ALU.mult
            )

        neg_max = keep.tile([P, 1], F32, name="neg_max")
        nc.vector.tensor_reduce(neg_max[:], score[:], AXIS.X, ALU.max, negate=True)
        total = keep.tile([P, 1], F32, name="total")
        nc.scalar.activation(p_pad[:, PAD:], score[:], ACT.Exp, bias=neg_max[:], accum_out=total[:])

        factors = keep.tile([P, 2], F32, name="factors")
        nc.gpsimd.memset(factors[:, 0:1], WEIGHT_SCALE)
        nc.gpsimd.tensor_scalar(factors[:, 1:2], smear_sb[:], smear_sb[:], WEIGHT_SCALE, ALU.mult, ALU.mult)
        inv_total = keep.tile([P, 1], F32, name="inv_total")
        normed = keep.tile([P, 2], F32, name="normed")
        near = slots_tile("near")
        near_part = [keep.tile([P, HALF], F32, name="near_part%d" % c) for c in range(2)]
        far_part = [keep.tile([P, HALF], F32, name="far_part%d" % c) for c in range(2)]

        def p_back(c, steps):
            return p_pad[:, PAD - steps + HALF * c : PAD - steps + HALF * (c + 1)]

        def make_near(c):
            nc.vector.scalar_tensor_tensor(near[:, halves[c]], p_back(c, 1), smear_sb[:], p_back(c, 0), ALU.mult, ALU.add)

        def scatter(c):
            nc.vector.tensor_tensor(
                placed[:].indirect(list1[:, list_halves[c]]), near_part[c][:], far_part[c][:], ALU.add
            )

        nc.vector.reciprocal(inv_total[:], total[:])
        make_near(0)
        nc.vector.tensor_scalar(far_part[0][:], p_back(0, SMEAR_REACH), inv_total[:], factors[:, 1:2], ALU.mult, ALU.mult)
        nc.vector.tensor_scalar(normed[:], factors[:], inv_total[:], None, ALU.mult)
        nc.vector.tensor_scalar(near_part[0][:], near[:, halves[0]], inv_total[:], WEIGHT_SCALE, ALU.mult, ALU.mult)
        make_near(1)
        scatter(0)
        nc.scalar.activation(near_part[1][:], near[:, halves[1]], ACT.Copy, scale=normed[:, 0:1])
        nc.scalar.activation(far_part[1][:], p_back(1, SMEAR_REACH), ACT.Copy, scale=normed[:, 1:2])
        scatter(1)

        width = T // STORES
        for c in range(STORES):
            columns = slice(width * c, width * (c + 1))
            result = keep.tile([P, width], F32, name="result%d" % c)
            nc.vector.scalar_tensor_tensor(
                result[:], old_sb[:, columns], fade_sb[:], placed[:, columns], ALU.mult, ALU.add
            )
            queue = nc.sync if c % 2 == 0 else nc.scalar
            queue.dma_start(out=out[:, columns], in_=result[:])
